import numpy as np
import ml_dtypes


def mxq(x, axis, fmt="e4m3"):
    dtype, down = {"e4m3": (ml_dtypes.float8_e4m3fn, 7), "e5m2": (ml_dtypes.float8_e5m2, 14)}[fmt]
    v = np.moveaxis(np.asarray(x, np.float32).astype(ml_dtypes.bfloat16).astype(np.float64), axis, -1)
    blocks = v.reshape(v.shape[:-1] + (-1, 32))
    amax = np.abs(blocks).max(-1, keepdims=True)
    byte = np.maximum(np.where(amax > 0, np.frexp(amax)[1] - 1 + 127, 0) - down, 1)
    scale = np.exp2(byte - 127.0)
    codes = (blocks / scale).astype(np.float32).astype(dtype).astype(np.float64)
    return np.moveaxis((codes * scale).reshape(v.shape), -1, axis)


WIDE = False


def mx_kscale(k):
    if not WIDE:
        return np.ones(k)
    levels = np.array([10, -10, 5, -5, 0])
    if k % 512:
        return np.exp2(np.random.permutation(np.resize(levels, k // 32))).repeat(32)
    a = np.empty((k // 512, 16))
    for p in range(k // 512):
        a[p, :8] = np.random.permutation(np.resize(levels, 8))
        for g in range(8):
            far = levels[np.abs(levels - a[p, g]) >= 10]
            a[p, g + 8] = far[np.random.randint(len(far))]
    return np.exp2(a.ravel()).repeat(32)


def f64(x):
    return np.asarray(x).astype(np.float64)


def striped(idx):
    return np.tile(idx.reshape(-1, 16).T, (8, 1)).astype(np.uint16)


def unstriped(offs):
    return offs[:16].T.reshape(-1).astype(np.int64)


K, T, S, N, U = 1024, 2048, 512, 128, 1024


def setup_inputs():
    n = np.random.standard_normal
    s = mx_kscale(K)[:, None]
    return {
        "xT": (n((K, T)) * s).astype(np.float32),
        "w1": (n((K, N)) / np.sqrt(K) / s).astype(np.float32),
        "scale": np.random.uniform(0.5, 1.5, (N, U)).astype(np.float32),
        "offs": striped(np.random.permutation(T)[:S]),
        "task": striped(np.random.permutation(U)[(U * np.random.uniform(0, 1, S) ** 4).astype(np.int64)]),
    }


def reference(xT, w1, scale, offs, task):
    xq = mxq(f64(xT)[:, unstriped(offs)], 0, "e4m3")
    y = mxq(f64(w1), 0, "e4m3").T @ xq
    g = f64(scale)[:, unstriped(task)]
    return y * g

@@ -1,0 +1,104 @@
+from contextlib import ExitStack
+
+import concourse.mybir as mybir
+
+K, T, S, N, U = 1024, 2048, 512, 128, 1024
+FLOPS = 2 * K * N * S
+
+F32 = mybir.dt.float32
+BF16 = mybir.dt.bfloat16
+U32 = mybir.dt.uint32
+U16 = mybir.dt.uint16
+U8 = mybir.dt.uint8
+FP8X4 = mybir.dt.float8_e4m3fn_x4
+
+P = 128
+PACK = 4
+K_PASS = P * PACK
+PASSES = K // K_PASS
+HALVES = 2
+HALF = S // HALVES
+LIST_COLS = HALF // 16
+
+
+def tile_picked_none_e_kernel(tc, xT, w1, scale, offs, task, out):
+    nc = tc.nc
+    with ExitStack() as ctx:
+        keep = ctx.enter_context(tc.tile_pool(name="keep", bufs=1))
+        psum = ctx.enter_context(tc.psum_pool(name="psum", bufs=1))
+
+        offs_sb = keep.tile([P, S // 16], U16, name="offs_sb")
+        task_sb = keep.tile([P, S // 16], U16, name="task_sb")
+        x_rows = xT.rearrange("(g p j) t -> g j p t", g=PASSES, j=PACK)
+        w_rows = w1.rearrange("(g p j) m -> g p j m", g=PASSES, j=PACK)
+
+        planes = {}
+        for g in range(PASSES):
+            for j in range(PACK):
+                planes[g, j] = keep.tile([P, T], F32, name="x_%d_%d" % (g, j))
+                nc.sync.dma_start(out=planes[g, j][:], in_=x_rows[g, j])
+                if (g, j) == (0, 0):
+                    nc.sync.dma_start(offs_sb[:], offs)
+                if (g, j) == (0, 1):
+                    nc.sync.dma_start(task_sb[:], task)
+        w_raw = []
+        for g in range(PASSES):
+            w_raw.append(keep.tile([P, PACK, N], F32, name="w_raw_%d" % g))
+            nc.sync.dma_start(out=w_raw[g][:], in_=w_rows[g])
+        scale_sb = keep.tile([P, U], F32, name="scale_sb")
+        nc.sync.dma_start(out=scale_sb[:], in_=scale)
+
+        x_codes, x_scales = {}, {}
+        for g in range(PASSES):
+            grouped = [keep.tile([P, HALF, PACK], BF16, name="x_grouped_%d_%d" % (g, h), align_bytes=64) for h in range(HALVES)]
+            for j in range(PACK):
+                for h in range(HALVES):
+                    nc.vector.tensor_copy(
+                        out=grouped[h][:, :, j],
+                        in_=planes[g, j][:].indirect(offs_sb[:, h * LIST_COLS : (h + 1) * LIST_COLS]),
+                    )
+            for h in range(HALVES):
+                x_codes[g, h] = keep.tile([P, HALF], U32, name="x_codes_%d_%d" % (g, h), align_bytes=64)
+                x_scales[g, h] = keep.tile([P, HALF], U8, name="x_scales_%d_%d" % (g, h), align_bytes=64)
+                nc.vector.quantize_mx(
+                    out=x_codes[g, h][:].bitcast(FP8X4),
+                    scales=x_scales[g, h][:],
+                    in_=grouped[h][:].rearrange("p n j -> p (n j)"),
+                )
+
+        w_codes, w_scales = [], []
+        for g in range(PASSES):
+            w_grouped = keep.tile([P, N, PACK], BF16, name="w_grouped_%d" % g, align_bytes=64)
+            nc.scalar.copy(out=w_grouped[:], in_=w_raw[g][:].rearrange("p j m -> p m j"))
+            w_codes.append(keep.tile([P, N], U32, name="w_codes_%d" % g, align_bytes=64))
+            w_scales.append(keep.tile([P, N], U8, name="w_scales_%d" % g, align_bytes=64))
+            nc.vector.quantize_mx(
+                out=w_codes[g][:].bitcast(FP8X4),
+                scales=w_scales[g][:],
+                in_=w_grouped[:].rearrange("p m j -> p (m j)"),
+            )
+
+        acc = [psum.tile([N, 512], F32, name="acc_%d" % h) for h in range(HALVES)]
+        for g in range(PASSES):
+            for h in range(HALVES):
+                nc.tensor.matmul_mx(
+                    out=acc[h][:, :HALF],
+                    lhsT=w_codes[g][:].bitcast(FP8X4),
+                    lhsT_scale=w_scales[g][:],
+                    rhs=x_codes[g, h][:].bitcast(FP8X4),
+                    rhs_scale=x_scales[g, h][:],
+                    start=(g == 0),
+                    stop=(g == PASSES - 1),
+                )
+
+        picked = []
+        for h in range(HALVES):
+            picked.append(keep.tile([N, HALF], F32, name="picked_scale_%d" % h))
+            nc.vector.tensor_copy(
+                out=picked[h][:],
+                in_=scale_sb[:].indirect(task_sb[:, h * LIST_COLS : (h + 1) * LIST_COLS]),
+            )
+        for h in range(HALVES):
+            result = keep.tile([N, HALF], F32, name="result_%d" % h)
+            nc.vector.tensor_tensor(result[:], acc[h][:, :HALF], picked[h][:], mybir.AluOpType.mult)
+            nc.sync.dma_start(out=out[:, h * HALF : (h + 1) * HALF], in_=result[:])

@@ -39,44 +39,56 @@ def tile_picked_none_e_kernel(tc, xT, w1, scale, offs, task, out):
                 nc.sync.dma_start(out=planes[g, j][:], in_=x_rows[g, j])
                 if (g, j) == (0, 0):
                     nc.sync.dma_start(offs_sb[:], offs)
-                if (g, j) == (0, 1):
-                    nc.sync.dma_start(task_sb[:], task)
+        nc.sync.dma_start(task_sb[:], task)
         w_raw = []
         for g in range(PASSES):
-            w_raw.append(keep.tile([P, PACK, N], F32, name="w_raw_%d" % g))
+            w_raw.append(keep.tile([P, PACK, N], F32, name="w_raw_%d" % g, tag="w_raw_%d" % g, align_bytes=64))
             nc.sync.dma_start(out=w_raw[g][:], in_=w_rows[g])
         scale_sb = keep.tile([P, U], F32, name="scale_sb")
         nc.sync.dma_start(out=scale_sb[:], in_=scale)
 
-        x_codes, x_scales = {}, {}
-        for g in range(PASSES):
-            grouped = [keep.tile([P, HALF, PACK], BF16, name="x_grouped_%d_%d" % (g, h), align_bytes=64) for h in range(HALVES)]
+        grouped, x_codes, x_scales, w_codes, w_scales = {}, {}, {}, {}, {}
+
+        def gather_tokens(g):
+            for h in range(HALVES):
+                grouped[g, h] = keep.tile([P, HALF, PACK], BF16, name="x_grouped_%d_%d" % (g, h), align_bytes=64)
             for j in range(PACK):
                 for h in range(HALVES):
                     nc.vector.tensor_copy(
-                        out=grouped[h][:, :, j],
+                        out=grouped[g, h][:, :, j],
                         in_=planes[g, j][:].indirect(offs_sb[:, h * LIST_COLS : (h + 1) * LIST_COLS]),
                     )
-            for h in range(HALVES):
-                x_codes[g, h] = keep.tile([P, HALF], U32, name="x_codes_%d_%d" % (g, h), align_bytes=64)
-                x_scales[g, h] = keep.tile([P, HALF], U8, name="x_scales_%d_%d" % (g, h), align_bytes=64)
-                nc.vector.quantize_mx(
-                    out=x_codes[g, h][:].bitcast(FP8X4),
-                    scales=x_scales[g, h][:],
-                    in_=grouped[h][:].rearrange("p n j -> p (n j)"),
-                )
 
-        w_codes, w_scales = [], []
-        for g in range(PASSES):
-            w_grouped = keep.tile([P, N, PACK], BF16, name="w_grouped_%d" % g, align_bytes=64)
-            nc.scalar.copy(out=w_grouped[:], in_=w_raw[g][:].rearrange("p j m -> p m j"))
-            w_codes.append(keep.tile([P, N], U32, name="w_codes_%d" % g, align_bytes=64))
-            w_scales.append(keep.tile([P, N], U8, name="w_scales_%d" % g, align_bytes=64))
+        def quantize_tokens(g, h, tag):
+            x_codes[g, h] = keep.tile([P, HALF], U32, name="x_codes_%d_%d" % (g, h), tag=tag, align_bytes=64)
+            x_scales[g, h] = keep.tile([P, HALF], U8, name="x_scales_%d_%d" % (g, h), align_bytes=64)
+            nc.vector.quantize_mx(
+                out=x_codes[g, h][:].bitcast(FP8X4),
+                scales=x_scales[g, h][:],
+                in_=grouped[g, h][:].rearrange("p n j -> p (n j)"),
+            )
+
+        def quantize_weights(g):
+            w_grouped = keep.tile([P, N, PACK], BF16, name="w_grouped_%d" % g, tag="w_grouped_%d" % g, align_bytes=64)
+            nc.scalar.copy(
+                out=w_grouped[:].rearrange("p (c i) j -> p c j i", i=4),
+                in_=w_raw[g][:].rearrange("p j (c i) -> p c j i", i=4),
+            )
+            w_codes[g] = keep.tile([P, N], U32, name="w_codes_%d" % g, align_bytes=64)
+            w_scales[g] = keep.tile([P, N], U8, name="w_scales_%d" % g, align_bytes=64)
             nc.vector.quantize_mx(
                 out=w_codes[g][:].bitcast(FP8X4),
                 scales=w_scales[g][:],
                 in_=w_grouped[:].rearrange("p m j -> p (m j)"),
             )
+
+        gather_tokens(0)
+        for h in range(HALVES):
+            quantize_tokens(0, h, "x_codes_first_%d" % h)
+        gather_tokens(1)
+        for h in range(HALVES):
+            quantize_weights(h)
+            quantize_tokens(1, h, "w_raw_%d" % h)
 
         acc = [psum.tile([N, 512], F32, name="acc_%d" % h) for h in range(HALVES)]
         for g in range(PASSES):
@@ -91,14 +103,13 @@ def tile_picked_none_e_kernel(tc, xT, w1, scale, offs, task, out):
                     stop=(g == PASSES - 1),
                 )
 
-        picked = []
+        picked = keep.tile([N, S], F32, name="picked_scale", tag="w_grouped_1", align_bytes=64)
         for h in range(HALVES):
-            picked.append(keep.tile([N, HALF], F32, name="picked_scale_%d" % h))
             nc.vector.tensor_copy(
-                out=picked[h][:],
+                out=picked[:, h * HALF : (h + 1) * HALF],
                 in_=scale_sb[:].indirect(task_sb[:, h * LIST_COLS : (h + 1) * LIST_COLS]),
             )
         for h in range(HALVES):
             result = keep.tile([N, HALF], F32, name="result_%d" % h)
-            nc.vector.tensor_tensor(result[:], acc[h][:, :HALF], picked[h][:], mybir.AluOpType.mult)
+            nc.vector.tensor_tensor(result[:], acc[h][:, :HALF], picked[:, h * HALF : (h + 1) * HALF], mybir.AluOpType.mult)
             nc.sync.dma_start(out=out[:, h * HALF : (h + 1) * HALF], in_=result[:])

@@ -29,34 +29,59 @@ def tile_picked_none_e_kernel(tc, xT, w1, scale, offs, task, out):
 
         offs_sb = keep.tile([P, S // 16], U16, name="offs_sb")
         task_sb = keep.tile([P, S // 16], U16, name="task_sb")
-        x_rows = xT.rearrange("(g p j) t -> g j p t", g=PASSES, j=PACK)
         w_rows = w1.rearrange("(g p j) m -> g p j m", g=PASSES, j=PACK)
 
+        x_view = xT.rearrange("(g p j) t -> p g j t", g=PASSES, j=PACK)
         planes = {}
+        first = keep.tile([P, 3, T], F32, name="x_first")
+        nc.sync.dma_start(out=first[:], in_=x_view[:, 0, 0:3, :])
+        nc.sync.dma_start(offs_sb[:], offs)
+        for j in range(3):
+            planes[0, j] = first[:, j, :]
+        second = keep.tile([P, PASSES, T], F32, name="x_second")
+        nc.sync.dma_start(out=second[:], in_=x_view[:, :, 3, :])
         for g in range(PASSES):
-            for j in range(PACK):
-                planes[g, j] = keep.tile([P, T], F32, name="x_%d_%d" % (g, j))
-                nc.sync.dma_start(out=planes[g, j][:], in_=x_rows[g, j])
-                if (g, j) == (0, 0):
-                    nc.sync.dma_start(offs_sb[:], offs)
-        nc.sync.dma_start(task_sb[:], task)
+            planes[g, 3] = second[:, g, :]
+        for j in (2, 0, 1):
+            single = keep.tile([P, T], F32, name="x_single_%d" % j)
+            nc.sync.dma_start(out=single[:], in_=x_view[:, 1, j, :])
+            planes[1, j] = single[:]
         w_raw = []
         for g in range(PASSES):
             w_raw.append(keep.tile([P, PACK, N], F32, name="w_raw_%d" % g, tag="w_raw_%d" % g, align_bytes=64))
             nc.sync.dma_start(out=w_raw[g][:], in_=w_rows[g])
+        nc.sync.dma_start(task_sb[:], task)
         scale_sb = keep.tile([P, U], F32, name="scale_sb")
         nc.sync.dma_start(out=scale_sb[:], in_=scale)
 
         grouped, x_codes, x_scales, w_codes, w_scales = {}, {}, {}, {}, {}
 
-        def gather_tokens(g):
+        def open_grouped(g):
             for h in range(HALVES):
-                grouped[g, h] = keep.tile([P, HALF, PACK], BF16, name="x_grouped_%d_%d" % (g, h), align_bytes=64)
-            for j in range(PACK):
+                grouped[g, h] = keep.tile(
+                    [P, HALF, PACK], BF16, name="x_grouped_%d_%d" % (g, h), tag="x_grouped_%d" % h, align_bytes=64
+                )
+
+        def gather_plain(g, js):
+            dense = [keep.tile([P, len(js), HALF], F32, name="x_dense_%d_%d" % (g, h)) for h in range(HALVES)]
+            for j in js:
+                for h in range(HALVES):
+                    nc.vector.tensor_copy(
+                        out=dense[h][:, j - min(js), :],
+                        in_=planes[g, j].indirect(offs_sb[:, h * LIST_COLS : (h + 1) * LIST_COLS]),
+                    )
+            for h in range(HALVES):
+                nc.scalar.copy(
+                    out=grouped[g, h][:, :, min(js) : max(js) + 1].rearrange("p (c i) j -> p c j i", i=4),
+                    in_=dense[h][:].rearrange("p j (c i) -> p c j i", i=4),
+                )
+
+        def gather_stepped(g, js):
+            for j in js:
                 for h in range(HALVES):
                     nc.vector.tensor_copy(
                         out=grouped[g, h][:, :, j],
-                        in_=planes[g, j][:].indirect(offs_sb[:, h * LIST_COLS : (h + 1) * LIST_COLS]),
+                        in_=planes[g, j].indirect(offs_sb[:, h * LIST_COLS : (h + 1) * LIST_COLS]),
                     )
 
         def quantize_tokens(g, h, tag):
@@ -82,10 +107,13 @@ def tile_picked_none_e_kernel(tc, xT, w1, scale, offs, task, out):
                 in_=w_grouped[:].rearrange("p m j -> p (m j)"),
             )
 
-        gather_tokens(0)
+        open_grouped(0)
+        gather_plain(0, (0, 1, 2, 3))
         for h in range(HALVES):
             quantize_tokens(0, h, "x_codes_first_%d" % h)
-        gather_tokens(1)
+        open_grouped(1)
+        gather_plain(1, (3, 2))
+        gather_stepped(1, (0, 1))
         for h in range(HALVES):
             quantize_weights(h)
             quantize_tokens(1, h, "w_raw_%d" % h)

@@ -11,6 +11,7 @@ U32 = mybir.dt.uint32
 U16 = mybir.dt.uint16
 U8 = mybir.dt.uint8
 FP8X4 = mybir.dt.float8_e4m3fn_x4
+COPY = mybir.ActivationFunctionType.Copy
 
 P = 128
 PACK = 4
@@ -76,13 +77,12 @@ def tile_picked_none_e_kernel(tc, xT, w1, scale, offs, task, out):
                     in_=dense[h][:].rearrange("p j (c i) -> p c j i", i=4),
                 )
 
-        def gather_stepped(g, js):
-            for j in js:
-                for h in range(HALVES):
-                    nc.vector.tensor_copy(
-                        out=grouped[g, h][:, :, j],
-                        in_=planes[g, j].indirect(offs_sb[:, h * LIST_COLS : (h + 1) * LIST_COLS]),
-                    )
+        def gather_stepped(g, j, halves):
+            for h in halves:
+                nc.vector.tensor_copy(
+                    out=grouped[g, h][:, :, j],
+                    in_=planes[g, j].indirect(offs_sb[:, h * LIST_COLS : (h + 1) * LIST_COLS]),
+                )
 
         def quantize_tokens(g, h, tag):
             x_codes[g, h] = keep.tile([P, HALF], U32, name="x_codes_%d_%d" % (g, h), tag=tag, align_bytes=64)
@@ -113,7 +113,11 @@ def tile_picked_none_e_kernel(tc, xT, w1, scale, offs, task, out):
             quantize_tokens(0, h, "x_codes_first_%d" % h)
         open_grouped(1)
         gather_plain(1, (3, 2))
-        gather_stepped(1, (0, 1))
+        gather_stepped(1, 0, (0, 1))
+        last_dense = keep.tile([P, HALF], BF16, name="x_last_dense")
+        nc.scalar.activation(last_dense[:], planes[1, 1].indirect(offs_sb[:, LIST_COLS:]), COPY)
+        gather_stepped(1, 1, (0,))
+        nc.vector.tensor_copy(out=grouped[1, 1][:, :, 1], in_=last_dense[:])
         for h in range(HALVES):
             quantize_weights(h)
             quantize_tokens(1, h, "w_raw_%d" % h)
@@ -131,13 +135,13 @@ def tile_picked_none_e_kernel(tc, xT, w1, scale, offs, task, out):
                     stop=(g == PASSES - 1),
                 )
 
-        picked = keep.tile([N, S], F32, name="picked_scale", tag="w_grouped_1", align_bytes=64)
-        for h in range(HALVES):
-            nc.vector.tensor_copy(
-                out=picked[:, h * HALF : (h + 1) * HALF],
-                in_=scale_sb[:].indirect(task_sb[:, h * LIST_COLS : (h + 1) * LIST_COLS]),
-            )
+        picked = [
+            keep.tile([N, HALF], F32, name="picked_scale_0"),
+            keep.tile([N, HALF], F32, name="picked_scale_1", tag="w_grouped_1", align_bytes=64),
+        ]
+        nc.scalar.activation(picked[0][:], scale_sb[:].indirect(task_sb[:, :LIST_COLS]), COPY)
+        nc.vector.tensor_copy(out=picked[1][:], in_=scale_sb[:].indirect(task_sb[:, LIST_COLS:]))
         for h in range(HALVES):
             result = keep.tile([N, HALF], F32, name="result_%d" % h)
-            nc.vector.tensor_tensor(result[:], acc[h][:, :HALF], picked[:, h * HALF : (h + 1) * HALF], mybir.AluOpType.mult)
+            nc.vector.tensor_tensor(result[:], acc[h][:, :HALF], picked[h][:], mybir.AluOpType.mult)
             nc.sync.dma_start(out=out[:, h * HALF : (h + 1) * HALF], in_=result[:])

@@ -20,6 +20,7 @@ PASSES = K // K_PASS
 HALVES = 2
 HALF = S // HALVES
 LIST_COLS = HALF // 16
+SCALAR_EXTRA = 64
 
 
 def tile_picked_none_e_kernel(tc, xT, w1, scale, offs, task, out):
@@ -139,8 +140,10 @@ def tile_picked_none_e_kernel(tc, xT, w1, scale, offs, task, out):
             keep.tile([N, HALF], F32, name="picked_scale_0"),
             keep.tile([N, HALF], F32, name="picked_scale_1", tag="w_grouped_1", align_bytes=64),
         ]
+        split = LIST_COLS + SCALAR_EXTRA // 16
         nc.scalar.activation(picked[0][:], scale_sb[:].indirect(task_sb[:, :LIST_COLS]), COPY)
-        nc.vector.tensor_copy(out=picked[1][:], in_=scale_sb[:].indirect(task_sb[:, LIST_COLS:]))
+        nc.scalar.activation(picked[1][:, :SCALAR_EXTRA], scale_sb[:].indirect(task_sb[:, LIST_COLS:split]), COPY)
+        nc.vector.tensor_copy(out=picked[1][:, SCALAR_EXTRA:], in_=scale_sb[:].indirect(task_sb[:, split:]))
         for h in range(HALVES):
             result = keep.tile([N, HALF], F32, name="result_%d" % h)
             nc.vector.tensor_tensor(result[:], acc[h][:, :HALF], picked[h][:], mybir.AluOpType.mult)

@@ -20,7 +20,9 @@ PASSES = K // K_PASS
 HALVES = 2
 HALF = S // HALVES
 LIST_COLS = HALF // 16
-SCALAR_EXTRA = 64
+QUARTERS = 4
+QUARTER = S // QUARTERS
+SCALAR_SHARE = 160
 
 
 def tile_picked_none_e_kernel(tc, xT, w1, scale, offs, task, out):
@@ -94,19 +96,30 @@ def tile_picked_none_e_kernel(tc, xT, w1, scale, offs, task, out):
                 in_=grouped[g, h][:].rearrange("p n j -> p (n j)"),
             )
 
-        def quantize_weights(g):
-            w_grouped = keep.tile([P, N, PACK], BF16, name="w_grouped_%d" % g, tag="w_grouped_%d" % g, align_bytes=64)
-            nc.scalar.copy(
-                out=w_grouped[:].rearrange("p (c i) j -> p c j i", i=4),
-                in_=w_raw[g][:].rearrange("p j (c i) -> p c j i", i=4),
-            )
+        def interleave_weights(g):
+            copies = (nc.vector.tensor_copy, nc.scalar.copy) if g == 1 else (nc.scalar.copy,)
+            width = N // len(copies)
             w_codes[g] = keep.tile([P, N], U32, name="w_codes_%d" % g, align_bytes=64)
             w_scales[g] = keep.tile([P, N], U8, name="w_scales_%d" % g, align_bytes=64)
-            nc.vector.quantize_mx(
-                out=w_codes[g][:].bitcast(FP8X4),
-                scales=w_scales[g][:],
-                in_=w_grouped[:].rearrange("p m j -> p (m j)"),
-            )
+            parts = []
+            for part, copy in enumerate(copies):
+                cols = slice(part * width, (part + 1) * width)
+                name = "w_grouped_%d_%d" % (g, part)
+                w_grouped = keep.tile([P, width, PACK], BF16, name=name, tag=name, align_bytes=64)
+                copy(
+                    out=w_grouped[:].rearrange("p (c i) j -> p c j i", i=4),
+                    in_=w_raw[g][:, :, cols].rearrange("p j (c i) -> p c j i", i=4),
+                )
+                parts.append((cols, w_grouped))
+            return parts
+
+        def quantize_weights(g, parts):
+            for cols, w_grouped in parts:
+                nc.vector.quantize_mx(
+                    out=w_codes[g][:, cols].bitcast(FP8X4),
+                    scales=w_scales[g][:, cols],
+                    in_=w_grouped[:].rearrange("p m j -> p (m j)"),
+                )
 
         open_grouped(0)
         gather_plain(0, (0, 1, 2, 3))
@@ -119,32 +132,39 @@ def tile_picked_none_e_kernel(tc, xT, w1, scale, offs, task, out):
         nc.scalar.activation(last_dense[:], planes[1, 1].indirect(offs_sb[:, LIST_COLS:]), COPY)
         gather_stepped(1, 1, (0,))
         nc.vector.tensor_copy(out=grouped[1, 1][:, :, 1], in_=last_dense[:])
+        w_parts = [interleave_weights(g) for g in range(PASSES)]
         for h in range(HALVES):
-            quantize_weights(h)
+            quantize_weights(h, w_parts[h])
             quantize_tokens(1, h, "w_raw_%d" % h)
 
-        acc = [psum.tile([N, 512], F32, name="acc_%d" % h) for h in range(HALVES)]
+        acc = [psum.tile([N, 512], F32, name="acc_%d" % q) for q in range(QUARTERS)]
         for g in range(PASSES):
-            for h in range(HALVES):
+            for q in range(QUARTERS):
+                cols = slice((q % 2) * QUARTER, (q % 2 + 1) * QUARTER)
                 nc.tensor.matmul_mx(
-                    out=acc[h][:, :HALF],
+                    out=acc[q][:, :QUARTER],
                     lhsT=w_codes[g][:].bitcast(FP8X4),
                     lhsT_scale=w_scales[g][:],
-                    rhs=x_codes[g, h][:].bitcast(FP8X4),
-                    rhs_scale=x_scales[g, h][:],
+                    rhs=x_codes[g, q // 2][:, cols].bitcast(FP8X4),
+                    rhs_scale=x_scales[g, q // 2][:, cols],
                     start=(g == 0),
                     stop=(g == PASSES - 1),
                 )
 
-        picked = [
-            keep.tile([N, HALF], F32, name="picked_scale_0"),
-            keep.tile([N, HALF], F32, name="picked_scale_1", tag="w_grouped_1", align_bytes=64),
-        ]
-        split = LIST_COLS + SCALAR_EXTRA // 16
-        nc.scalar.activation(picked[0][:], scale_sb[:].indirect(task_sb[:, :LIST_COLS]), COPY)
-        nc.scalar.activation(picked[1][:, :SCALAR_EXTRA], scale_sb[:].indirect(task_sb[:, LIST_COLS:split]), COPY)
-        nc.vector.tensor_copy(out=picked[1][:, SCALAR_EXTRA:], in_=scale_sb[:].indirect(task_sb[:, split:]))
+        picked = keep.tile([N, S], F32, name="picked_scale", tag="w_grouped_1_1", align_bytes=64)
+
+        def task_cols(start, stop):
+            return task_sb[:, start // 16 : stop // 16]
+
+        lo, hi = SCALAR_SHARE, S - SCALAR_SHARE
+        nc.scalar.activation(picked[:, :lo], scale_sb[:].indirect(task_cols(0, lo)), COPY)
+        nc.scalar.activation(picked[:, hi:], scale_sb[:].indirect(task_cols(hi, S)), COPY)
+        nc.vector.tensor_copy(out=picked[:, lo:hi], in_=scale_sb[:].indirect(task_cols(lo, hi)))
         for h in range(HALVES):
             result = keep.tile([N, HALF], F32, name="result_%d" % h)
-            nc.vector.tensor_tensor(result[:], acc[h][:, :HALF], picked[h][:], mybir.AluOpType.mult)
+            for part in range(2):
+                cols = slice(part * QUARTER, (part + 1) * QUARTER)
+                nc.vector.tensor_tensor(
+                    result[:, cols], acc[2 * h + part][:, :QUARTER], picked[:, h * HALF : (h + 1) * HALF][:, cols], mybir.AluOpType.mult
+                )
             nc.sync.dma_start(out=out[:, h * HALF : (h + 1) * HALF], in_=result[:])

@@ -138,18 +138,20 @@ def tile_picked_none_e_kernel(tc, xT, w1, scale, offs, task, out):
             quantize_tokens(1, h, "w_raw_%d" % h)
 
         acc = [psum.tile([N, 512], F32, name="acc_%d" % q) for q in range(QUARTERS)]
-        for g in range(PASSES):
-            for q in range(QUARTERS):
-                cols = slice((q % 2) * QUARTER, (q % 2 + 1) * QUARTER)
-                nc.tensor.matmul_mx(
-                    out=acc[q][:, :QUARTER],
-                    lhsT=w_codes[g][:].bitcast(FP8X4),
-                    lhsT_scale=w_scales[g][:],
-                    rhs=x_codes[g, q // 2][:, cols].bitcast(FP8X4),
-                    rhs_scale=x_scales[g, q // 2][:, cols],
-                    start=(g == 0),
-                    stop=(g == PASSES - 1),
-                )
+        final = QUARTERS - 1
+        order = [(0, q) for q in range(final)] + [(1, q) for q in range(QUARTERS)] + [(0, final)]
+        for g, q in order:
+            cols = slice((q % 2) * QUARTER, (q % 2 + 1) * QUARTER)
+            opens = (g == 1) if q == final else (g == 0)
+            nc.tensor.matmul_mx(
+                out=acc[q][:, :QUARTER],
+                lhsT=w_codes[g][:].bitcast(FP8X4),
+                lhsT_scale=w_scales[g][:],
+                rhs=x_codes[g, q // 2][:, cols].bitcast(FP8X4),
+                rhs_scale=x_scales[g, q // 2][:, cols],
+                start=opens,
+                stop=not opens,
+            )
 
         picked = keep.tile([N, S], F32, name="picked_scale", tag="w_grouped_1_1", align_bytes=64)
 

@@ -61,10 +61,9 @@ def tile_picked_none_e_kernel(tc, xT, w1, scale, offs, task, out):
         grouped, x_codes, x_scales, w_codes, w_scales = {}, {}, {}, {}, {}
 
         def open_grouped(g):
+            grouped[g] = keep.tile([P, S, PACK], BF16, name="x_grouped_%d" % g, align_bytes=64)
             for h in range(HALVES):
-                grouped[g, h] = keep.tile(
-                    [P, HALF, PACK], BF16, name="x_grouped_%d_%d" % (g, h), tag="x_grouped_%d" % h, align_bytes=64
-                )
+                grouped[g, h] = grouped[g][:, h * HALF : (h + 1) * HALF, :]
 
         def gather_plain(g, js):
             dense = [keep.tile([P, len(js), HALF], F32, name="x_dense_%d_%d" % (g, h)) for h in range(HALVES)]
@@ -93,11 +92,11 @@ def tile_picked_none_e_kernel(tc, xT, w1, scale, offs, task, out):
             nc.vector.quantize_mx(
                 out=x_codes[g, h][:].bitcast(FP8X4),
                 scales=x_scales[g, h][:],
-                in_=grouped[g, h][:].rearrange("p n j -> p (n j)"),
+                in_=grouped[g, h].rearrange("p n j -> p (n j)"),
             )
 
         def interleave_weights(g):
-            copies = (nc.vector.tensor_copy, nc.scalar.copy) if g == 1 else (nc.scalar.copy,)
+            copies = (nc.scalar.copy,)
             width = N // len(copies)
             w_codes[g] = keep.tile([P, N], U32, name="w_codes_%d" % g, align_bytes=64)
             w_scales[g] = keep.tile([P, N], U8, name="w_scales_%d" % g, align_bytes=64)
@@ -128,10 +127,11 @@ def tile_picked_none_e_kernel(tc, xT, w1, scale, offs, task, out):
         open_grouped(1)
         gather_plain(1, (3, 2))
         gather_stepped(1, 0, (0, 1))
-        last_dense = keep.tile([P, HALF], BF16, name="x_last_dense")
-        nc.scalar.activation(last_dense[:], planes[1, 1].indirect(offs_sb[:, LIST_COLS:]), COPY)
-        gather_stepped(1, 1, (0,))
-        nc.vector.tensor_copy(out=grouped[1, 1][:, :, 1], in_=last_dense[:])
+        cut = S - QUARTER
+        last_dense = keep.tile([P, QUARTER], BF16, name="x_last_dense")
+        nc.scalar.activation(last_dense[:], planes[1, 1].indirect(offs_sb[:, cut // 16 :]), COPY)
+        nc.vector.tensor_copy(out=grouped[1][:, :cut, 1], in_=planes[1, 1].indirect(offs_sb[:, : cut // 16]))
+        nc.vector.tensor_copy(out=grouped[1][:, cut:, 1], in_=last_dense[:])
         w_parts = [interleave_weights(g) for g in range(PASSES)]
         for h in range(HALVES):
             quantize_weights(h, w_parts[h])
@@ -153,7 +153,7 @@ def tile_picked_none_e_kernel(tc, xT, w1, scale, offs, task, out):
                 stop=not opens,
             )
 
-        picked = keep.tile([N, S], F32, name="picked_scale", tag="w_grouped_1_1", align_bytes=64)
+        picked = keep.tile([N, S], F32, name="picked_scale", tag="w_grouped_1_0", align_bytes=64)
 
         def task_cols(start, stop):
             return task_sb[:, start // 16 : stop // 16]

@@ -65,14 +65,15 @@ def tile_picked_none_e_kernel(tc, xT, w1, scale, offs, task, out):
             for h in range(HALVES):
                 grouped[g, h] = grouped[g][:, h * HALF : (h + 1) * HALF, :]
 
-        def gather_plain(g, js):
-            dense = [keep.tile([P, len(js), HALF], F32, name="x_dense_%d_%d" % (g, h)) for h in range(HALVES)]
+        def gather_plain(g, js, on_scalar=()):
+            dense = [keep.tile([P, len(js), HALF], F32, name="x_dense_%d_%d_%d" % (g, min(js), h)) for h in range(HALVES)]
             for j in js:
                 for h in range(HALVES):
-                    nc.vector.tensor_copy(
-                        out=dense[h][:, j - min(js), :],
-                        in_=planes[g, j].indirect(offs_sb[:, h * LIST_COLS : (h + 1) * LIST_COLS]),
-                    )
+                    window = planes[g, j].indirect(offs_sb[:, h * LIST_COLS : (h + 1) * LIST_COLS])
+                    if (j, h) in on_scalar:
+                        nc.scalar.activation(dense[h][:, j - min(js), :], window, COPY)
+                    else:
+                        nc.vector.tensor_copy(out=dense[h][:, j - min(js), :], in_=window)
             for h in range(HALVES):
                 nc.scalar.copy(
                     out=grouped[g, h][:, :, min(js) : max(js) + 1].rearrange("p (c i) j -> p c j i", i=4),
@@ -121,11 +122,12 @@ def tile_picked_none_e_kernel(tc, xT, w1, scale, offs, task, out):
                 )
 
         open_grouped(0)
-        gather_plain(0, (0, 1, 2, 3))
+        gather_plain(0, (0, 1))
+        gather_plain(0, (2, 3))
         for h in range(HALVES):
             quantize_tokens(0, h, "x_codes_first_%d" % h)
         open_grouped(1)
-        gather_plain(1, (3, 2))
+        gather_plain(1, (3, 2), on_scalar=((3, 1),))
         gather_stepped(1, 0, (0, 1))
         cut = S - QUARTER
         last_dense = keep.tile([P, QUARTER], BF16, name="x_last_dense")

@@ -37,16 +37,13 @@ def tile_picked_none_e_kernel(tc, xT, w1, scale, offs, task, out):
 
         x_view = xT.rearrange("(g p j) t -> p g j t", g=PASSES, j=PACK)
         planes = {}
-        first = keep.tile([P, 3, T], F32, name="x_first")
-        nc.sync.dma_start(out=first[:], in_=x_view[:, 0, 0:3, :])
-        nc.sync.dma_start(offs_sb[:], offs)
-        for j in range(3):
-            planes[0, j] = first[:, j, :]
-        second = keep.tile([P, PASSES, T], F32, name="x_second")
-        nc.sync.dma_start(out=second[:], in_=x_view[:, :, 3, :])
-        for g in range(PASSES):
-            planes[g, 3] = second[:, g, :]
-        for j in (2, 0, 1):
+        for g, j in ((0, 0), (0, 2), (1, 2)):
+            pair = keep.tile([P, 2, T], F32, name="x_pair_%d_%d" % (g, j))
+            nc.sync.dma_start(out=pair[:], in_=x_view[:, g, j : j + 2, :])
+            planes[g, j], planes[g, j + 1] = pair[:, 0, :], pair[:, 1, :]
+            if (g, j) == (0, 0):
+                nc.sync.dma_start(offs_sb[:], offs)
+        for j in (0, 1):
             single = keep.tile([P, T], F32, name="x_single_%d" % j)
             nc.sync.dma_start(out=single[:], in_=x_view[:, 1, j, :])
             planes[1, j] = single[:]

from contextlib import ExitStack

import concourse.mybir as mybir

K, T, S, N, U = 1024, 2048, 512, 128, 1024
FLOPS = 2 * K * N * S

F32 = mybir.dt.float32
BF16 = mybir.dt.bfloat16
U32 = mybir.dt.uint32
U16 = mybir.dt.uint16
U8 = mybir.dt.uint8
FP8X4 = mybir.dt.float8_e4m3fn_x4
COPY = mybir.ActivationFunctionType.Copy

P = 128
PACK = 4
K_PASS = P * PACK
PASSES = K // K_PASS
HALVES = 2
HALF = S // HALVES
LIST_COLS = HALF // 16
QUARTERS = 4
QUARTER = S // QUARTERS
SCALAR_SHARE = 160


def tile_picked_none_e_kernel(tc, xT, w1, scale, offs, task, out):
    nc = tc.nc
    with ExitStack() as ctx:
        keep = ctx.enter_context(tc.tile_pool(name="keep", bufs=1))
        psum = ctx.enter_context(tc.psum_pool(name="psum", bufs=1))

        offs_sb = keep.tile([P, S // 16], U16, name="offs_sb")
        task_sb = keep.tile([P, S // 16], U16, name="task_sb")
        w_rows = w1.rearrange("(g p j) m -> g p j m", g=PASSES, j=PACK)

        x_view = xT.rearrange("(g p j) t -> p g j t", g=PASSES, j=PACK)
        planes = {}
        for g, j in ((0, 0), (0, 2), (1, 2)):
            pair = keep.tile([P, 2, T], F32, name="x_pair_%d_%d" % (g, j))
            nc.sync.dma_start(out=pair[:], in_=x_view[:, g, j : j + 2, :])
            planes[g, j], planes[g, j + 1] = pair[:, 0, :], pair[:, 1, :]
            if (g, j) == (0, 0):
                nc.sync.dma_start(offs_sb[:], offs)
        for j in (0, 1):
            single = keep.tile([P, T], F32, name="x_single_%d" % j)
            nc.sync.dma_start(out=single[:], in_=x_view[:, 1, j, :])
            planes[1, j] = single[:]
        w_raw = []
        for g in range(PASSES):
            w_raw.append(keep.tile([P, PACK, N], F32, name="w_raw_%d" % g, tag="w_raw_%d" % g, align_bytes=64))
            nc.sync.dma_start(out=w_raw[g][:], in_=w_rows[g])
        nc.sync.dma_start(task_sb[:], task)
        scale_sb = keep.tile([P, U], F32, name="scale_sb")
        nc.sync.dma_start(out=scale_sb[:], in_=scale)

        grouped, x_codes, x_scales, w_codes, w_scales = {}, {}, {}, {}, {}

        def open_grouped(g):
            grouped[g] = keep.tile([P, S, PACK], BF16, name="x_grouped_%d" % g, align_bytes=64)
            for h in range(HALVES):
                grouped[g, h] = grouped[g][:, h * HALF : (h + 1) * HALF, :]

        def gather_plain(g, js, on_scalar=()):
            dense = [keep.tile([P, len(js), HALF], F32, name="x_dense_%d_%d_%d" % (g, min(js), h)) for h in range(HALVES)]
            for j in js:
                for h in range(HALVES):
                    window = planes[g, j].indirect(offs_sb[:, h * LIST_COLS : (h + 1) * LIST_COLS])
                    if (j, h) in on_scalar:
                        nc.scalar.activation(dense[h][:, j - min(js), :], window, COPY)
                    else:
                        nc.vector.tensor_copy(out=dense[h][:, j - min(js), :], in_=window)
            for h in range(HALVES):
                nc.scalar.copy(
                    out=grouped[g, h][:, :, min(js) : max(js) + 1].rearrange("p (c i) j -> p c j i", i=4),
                    in_=dense[h][:].rearrange("p j (c i) -> p c j i", i=4),
                )

        def gather_stepped(g, j, halves):
            for h in halves:
                nc.vector.tensor_copy(
                    out=grouped[g, h][:, :, j],
                    in_=planes[g, j].indirect(offs_sb[:, h * LIST_COLS : (h + 1) * LIST_COLS]),
                )

        def quantize_tokens(g, h, tag):
            x_codes[g, h] = keep.tile([P, HALF], U32, name="x_codes_%d_%d" % (g, h), tag=tag, align_bytes=64)
            x_scales[g, h] = keep.tile([P, HALF], U8, name="x_scales_%d_%d" % (g, h), align_bytes=64)
            nc.vector.quantize_mx(
                out=x_codes[g, h][:].bitcast(FP8X4),
                scales=x_scales[g, h][:],
                in_=grouped[g, h].rearrange("p n j -> p (n j)"),
            )

        def interleave_weights(g):
            copies = (nc.scalar.copy,)
            width = N // len(copies)
            w_codes[g] = keep.tile([P, N], U32, name="w_codes_%d" % g, align_bytes=64)
            w_scales[g] = keep.tile([P, N], U8, name="w_scales_%d" % g, align_bytes=64)
            parts = []
            for part, copy in enumerate(copies):
                cols = slice(part * width, (part + 1) * width)
                name = "w_grouped_%d_%d" % (g, part)
                w_grouped = keep.tile([P, width, PACK], BF16, name=name, tag=name, align_bytes=64)
                copy(
                    out=w_grouped[:].rearrange("p (c i) j -> p c j i", i=4),
                    in_=w_raw[g][:, :, cols].rearrange("p j (c i) -> p c j i", i=4),
                )
                parts.append((cols, w_grouped))
            return parts

        def quantize_weights(g, parts):
            for cols, w_grouped in parts:
                nc.vector.quantize_mx(
                    out=w_codes[g][:, cols].bitcast(FP8X4),
                    scales=w_scales[g][:, cols],
                    in_=w_grouped[:].rearrange("p m j -> p (m j)"),
                )

        open_grouped(0)
        gather_plain(0, (0, 1))
        gather_plain(0, (2, 3))
        for h in range(HALVES):
            quantize_tokens(0, h, "x_codes_first_%d" % h)
        open_grouped(1)
        gather_plain(1, (3, 2), on_scalar=((3, 1),))
        gather_stepped(1, 0, (0, 1))
        cut = S - QUARTER
        last_dense = keep.tile([P, QUARTER], BF16, name="x_last_dense")
        nc.scalar.activation(last_dense[:], planes[1, 1].indirect(offs_sb[:, cut // 16 :]), COPY)
        nc.vector.tensor_copy(out=grouped[1][:, :cut, 1], in_=planes[1, 1].indirect(offs_sb[:, : cut // 16]))
        nc.vector.tensor_copy(out=grouped[1][:, cut:, 1], in_=last_dense[:])
        w_parts = [interleave_weights(g) for g in range(PASSES)]
        for h in range(HALVES):
            quantize_weights(h, w_parts[h])
            quantize_tokens(1, h, "w_raw_%d" % h)

        acc = [psum.tile([N, 512], F32, name="acc_%d" % q) for q in range(QUARTERS)]
        final = QUARTERS - 1
        order = [(0, q) for q in range(final)] + [(1, q) for q in range(QUARTERS)] + [(0, final)]
        for g, q in order:
            cols = slice((q % 2) * QUARTER, (q % 2 + 1) * QUARTER)
            opens = (g == 1) if q == final else (g == 0)
            nc.tensor.matmul_mx(
                out=acc[q][:, :QUARTER],
                lhsT=w_codes[g][:].bitcast(FP8X4),
                lhsT_scale=w_scales[g][:],
                rhs=x_codes[g, q // 2][:, cols].bitcast(FP8X4),
                rhs_scale=x_scales[g, q // 2][:, cols],
                start=opens,
                stop=not opens,
            )

        picked = keep.tile([N, S], F32, name="picked_scale", tag="w_grouped_1_0", align_bytes=64)

        def task_cols(start, stop):
            return task_sb[:, start // 16 : stop // 16]

        lo, hi = SCALAR_SHARE, S - SCALAR_SHARE
        nc.scalar.activation(picked[:, :lo], scale_sb[:].indirect(task_cols(0, lo)), COPY)
        nc.scalar.activation(picked[:, hi:], scale_sb[:].indirect(task_cols(hi, S)), COPY)
        nc.vector.tensor_copy(out=picked[:, lo:hi], in_=scale_sb[:].indirect(task_cols(lo, hi)))
        for h in range(HALVES):
            result = keep.tile([N, HALF], F32, name="result_%d" % h)
            for part in range(2):
                cols = slice(part * QUARTER, (part + 1) * QUARTER)
                nc.vector.tensor_tensor(
                    result[:, cols], acc[2 * h + part][:, :QUARTER], picked[:, h * HALF : (h + 1) * HALF][:, cols], mybir.AluOpType.mult
                )
            nc.sync.dma_start(out=out[:, h * HALF : (h + 1) * HALF], in_=result[:])
